import numpy as np
CORES = [2,3,0,1]
N = 4
COUNTS = [[0,37,5,90],[64,0,2,11],[7,19,0,30],[128,3,44,0]]
XW, YW = 175, 199
def setup_inputs(rng):
    return {"x": rng.standard_normal((N, 128, XW), dtype=np.float32)}
def reference(x):
    y = np.full((N, 128, YW), np.nan, x.dtype)
    fill = [0] * N
    for s in range(N):
        o = 0
        for d in range(N):
            c = COUNTS[s][d]
            y[d][:, fill[d]:fill[d] + c] = x[s][:, o:o + c]
            o += c; fill[d] += c
    return {"y": y}

SCRATCH = {
    "send": ("sbuf", [128, 175], "float32"),
    "land": ("sbuf", [128, 199], "float32"),
}
SEMAPHORES = ["loaded", "read", "arrived", "stored"]

ENGINES = 16


def rank_program(g, core, T, topo):
    rank = T.rank_of(core)
    if rank is None:
        return
    counts = T.tables["COUNTS"]
    n = len(T.cores)

    out_total = sum(counts[rank][d] for d in range(n) if d != rank)
    in_total = sum(counts[s][rank] for s in range(n) if s != rank)

    if out_total:
        g.dma_start(T.send[:, 0:out_total], T.x[:, 0:out_total]).then_inc(T.sem.loaded, 16)
        g.wait_ge(T.sem.loaded, 16)

    sent = 0
    xoff = 0
    for d in range(n):
        c = counts[rank][d] if d != rank else 0
        if c == 0:
            continue
        yoff = sum(counts[s][d] for s in range(rank) if s != d)
        dst = T.cores[d]
        rid, pid = topo.addr(dst)[0:2]
        g.remote_dma(
            T.land[:, yoff:yoff + c],
            T.send[:, xoff:xoff + c],
            T.sem.arrived,
            T.sem.read,
            pid,
            rid,
            topo.mask(core, dst),
        )
        sent += 1
        xoff += c

    incoming = sum(1 for s in range(n) if s != rank and counts[s][rank] > 0)
    if incoming:
        g.wait_ge(T.sem.arrived, ENGINES * incoming)
        g.dma_start(T.y[:, 0:in_total], T.land[:, 0:in_total]).then_inc(T.sem.stored, 16)
        g.wait_ge(T.sem.stored, 16)

    if sent:
        g.wait_ge(T.sem.read, ENGINES * sent)
